import numpy as np
import ml_dtypes


def mxq(x, axis, fmt="e4m3"):
    dtype, down = {"e4m3": (ml_dtypes.float8_e4m3fn, 7), "e5m2": (ml_dtypes.float8_e5m2, 14)}[fmt]
    v = np.moveaxis(np.asarray(x, np.float32).astype(ml_dtypes.bfloat16).astype(np.float64), axis, -1)
    blocks = v.reshape(v.shape[:-1] + (-1, 32))
    amax = np.abs(blocks).max(-1, keepdims=True)
    byte = np.maximum(np.where(amax > 0, np.frexp(amax)[1] - 1 + 127, 0) - down, 1)
    scale = np.exp2(byte - 127.0)
    codes = (blocks / scale).astype(np.float32).astype(dtype).astype(np.float64)
    return np.moveaxis((codes * scale).reshape(v.shape), -1, axis)


WIDE = False


def mx_kscale(k):
    if not WIDE:
        return np.ones(k)
    levels = np.array([10, -10, 5, -5, 0])
    if k % 512:
        return np.exp2(np.random.permutation(np.resize(levels, k // 32))).repeat(32)
    a = np.empty((k // 512, 16))
    for p in range(k // 512):
        a[p, :8] = np.random.permutation(np.resize(levels, 8))
        for g in range(8):
            far = levels[np.abs(levels - a[p, g]) >= 10]
            a[p, g + 8] = far[np.random.randint(len(far))]
    return np.exp2(a.ravel()).repeat(32)


BF16 = ml_dtypes.bfloat16


def bf(x):
    return np.asarray(x, np.float32).astype(BF16)


def f64(x):
    return np.asarray(x).astype(np.float64)


B, D, K, M = 2048, 1024, 512, 512


def stable_softmax(z):
    e = np.exp(z - np.max(z, axis=-1, keepdims=True))
    return e / np.sum(e, axis=-1, keepdims=True)


def stable_logsumexp(z):
    top = np.max(z, axis=-1, keepdims=True)
    return top + np.log(np.sum(np.exp(z - top), axis=-1, keepdims=True))


def draw0():
    s, r = mx_kscale(D), mx_kscale(K)
    return {
        "x": bf(np.random.standard_normal((B, D)) * s[None, :]),
        "c1": bf(np.random.standard_normal((K, D)) / np.sqrt(D) / s[None, :]),
        "v1": bf(0.5 * np.random.standard_normal((K, D)) * s[None, :] / r[:, None]),
        "c2": bf(np.random.standard_normal((M, D)) / np.sqrt(D) / s[None, :]),
        "g": bf(4.0 * np.random.standard_normal(K) * r),
        "b1": bf(0.5 * np.random.standard_normal(K)),
        "b2": bf(0.5 * np.random.standard_normal(M)),
    }


def core(x, c1, v1, c2, g, b1, b2):
    xq = mxq(f64(x), 1, "e4m3")
    c2q = mxq(f64(c2), 1, "e4m3")
    s1 = xq @ mxq(f64(c1), 1, "e4m3").T
    s2 = xq @ c2q.T
    cross = mxq(f64(v1), 1, "e4m3") @ c2q.T
    p1 = stable_softmax(2.0 * s1 + f64(b1)[None, :])
    a = p1 * f64(g)[None, :]
    t = mxq(a, 1, "e4m3") @ mxq(cross, 0, "e4m3")
    l2 = s2 - t + f64(b2)[None, :]
    log_m = np.log(c2.shape[0])
    return l2 - stable_logsumexp(l2) + log_m


def e4m3fn_bytes(y):
    return np.clip(np.asarray(y, np.float64), -448.0, 448.0).astype(np.float32).astype(ml_dtypes.float8_e4m3fn).view(np.uint8)


def e4m3fn_values(b):
    return np.asarray(b, np.uint8).view(ml_dtypes.float8_e4m3fn).astype(np.float64)


def setup_inputs():
    d = draw0()
    x0 = np.asarray(d['x']).astype(np.float64)
    s = (np.max(np.abs(x0), axis=(0,), keepdims=True) / 448.0).astype(np.float32)
    out = {}
    for k, v in d.items():
        if k == 'x':
            out['x_bytes'] = e4m3fn_bytes(x0 / s.astype(np.float64))
            out['x_scale'] = s
        else:
            out[k] = v
    return out


def reference(x_bytes, x_scale, c1, v1, c2, g, b1, b2):
    return core(e4m3fn_values(x_bytes) * x_scale.astype(np.float64), c1, v1, c2, g, b1, b2)

@@ -1,0 +1,345 @@
+from contextlib import ExitStack
+
+import concourse.mybir as mybir
+from concourse.masks import make_identity
+
+B, D, K, M = 2048, 1024, 512, 512
+FLOPS = 2 * B * D * (K + M) + 2 * K * M * D + 2 * B * K * M
+
+F32 = mybir.dt.float32
+BF16 = mybir.dt.bfloat16
+U32 = mybir.dt.uint32
+U8 = mybir.dt.uint8
+FP8 = mybir.dt.float8_e4m3fn
+FP8X4 = mybir.dt.float8_e4m3fn_x4
+ACT = mybir.ActivationFunctionType
+ALU = mybir.AluOpType
+AX = mybir.AxisListType
+
+P = 128
+NT = B // P
+G = D // 512
+
+ORDER = "OKFGBHJPELDNQIMCR"
+OFFSET = {"B": 0, "C": 1, "D": 2, "E": 3, "F": 5, "G": 5, "H": 6, "I": 6, "J": 7,
+          "K": 9, "L": 9, "M": 9, "N": 10, "O": 12, "P": 12, "Q": 12, "R": 12}
+HEAD = {
+    2: ["c1T0", "c1T1", "c1T2", "c1T3"],
+    3: ["c1e0s", "c1e1v", "c1e2s", "c1e3v", "c2T0", "c2T1", "c2e0s", "c2e1s"],
+    4: ["c1q0", "c1q1", "c1q2", "c1q3", "c2T2", "c2T3", "c2e2s", "c2e3s"],
+    5: ["v1T0", "v1T1", "v1e0s", "v1e1s"],
+    6: ["c2q0", "c2q1", "v1q0", "v1q1", "v1T2", "v1T3", "v1e2s", "v1e3s"],
+    7: ["gb"],
+    8: ["v1q2", "v1q3"],
+    9: ["crm0", "cre0s"],
+    10: ["crm1", "cre1s", "crm2", "cre2s"],
+    11: ["crm3", "cre3s"],
+    12: ["crq"],
+}
+GROUPS = (9, 15)
+
+
+def tile_softresidualsemanticids_kernel(tc, x_bytes, x_scale, c1, v1, c2, g, b1, b2, out):
+    nc = tc.nc
+    with ExitStack() as ctx:
+        keep = ctx.enter_context(tc.tile_pool(name="keep", bufs=1))
+        work = ctx.enter_context(tc.tile_pool(name="work", bufs=3))
+        psum = ctx.enter_context(tc.psum_pool(name="psum", bufs=1))
+
+        ident = keep.tile([P, P], F32, name="ident")
+        ones = keep.tile([P, P], BF16, name="ones")
+        rows_gb = keep.tile([P, 2, K], BF16, name="rows_gb")
+        rows_b1 = keep.tile([P, P], BF16, name="rows_b1")
+        rows_b1f = keep.tile([P, P], F32, name="rows_b1f")
+        neg_b1 = keep.tile([P, 4], F32, name="neg_b1")
+        neg_g = keep.tile([P, K], BF16, name="neg_g")
+        b2_all = keep.tile([P, M], BF16, name="b2_all")
+        scale_all = keep.tile([P, D], F32, name="scale_all")
+        warm = keep.tile([P, 1], F32, name="warm")
+        xb = [keep.tile([P, D], U8, name="xb%d" % i) for i in range(4)]
+        xq4 = [keep.tile([P, 4, D], U8, name="xbq%d" % i) for i in range(3)]
+        raw = {}
+        for n in ("c1", "c2", "v1"):
+            raw[n] = keep.tile([P, 4, D], BF16, name="raw_" + n)
+        grp = {}
+        codes = {}
+        scl = {}
+        for n in ("c1", "v1"):
+            grp[n] = [keep.tile([P, G * P * 4], BF16, name="grp_%s%d" % (n, j), align_bytes=64) for j in range(4)]
+            codes[n] = [keep.tile([P, G * P], U32, name="codes_%s%d" % (n, j), align_bytes=64) for j in range(4)]
+            scl[n] = [keep.tile([P, G * P], U8, name="scl_%s%d" % (n, j), align_bytes=64) for j in range(4)]
+        grp["c2"] = keep.tile([P, G, M, 4], BF16, name="grp_c2", align_bytes=64)
+        codes["c2"] = [keep.tile([P, M], U32, name="codes_c2%d" % j, align_bytes=64) for j in range(G)]
+        scl["c2"] = [keep.tile([P, M], U8, name="scl_c2%d" % j, align_bytes=64) for j in range(G)]
+        grp_cr = keep.tile([P, M, 4], BF16, name="grp_cr", align_bytes=64)
+        codes_cr = keep.tile([P, M], U32, name="codes_cr", align_bytes=64)
+        scl_cr = keep.tile([P, M], U8, name="scl_cr", align_bytes=64)
+        ny = [keep.tile([P, M], F32, name="ny%d" % i) for i in range(NT)]
+        sum2 = {}
+        min2 = {}
+        lns = {}
+        shift = {}
+        lo = 0
+        for hi in GROUPS:
+            n = hi + 1 - lo
+            sum2[hi] = keep.tile([P, n], F32, name="sum2_%d" % hi)
+            min2[hi] = keep.tile([P, n], F32, name="min2_%d" % hi)
+            lns[hi] = keep.tile([P, n], F32, name="lns_%d" % hi)
+            shift[hi] = keep.tile([P, n], F32, name="shift_%d" % hi)
+            lo = hi + 1
+
+        def group(i):
+            lo = 0
+            for hi in GROUPS:
+                if i <= hi:
+                    return hi, i - lo
+                lo = hi + 1
+
+        def x_rows(i):
+            if i < 4:
+                return xb[i][:]
+            return xq4[i // 4 - 1][:, i % 4, :]
+
+        with tc.manual_schedule():
+            nc.gpsimd.memset(rows_gb[:], 0.0)
+            nc.gpsimd.memset(rows_b1[:], 0.0)
+            nc.gpsimd.memset(ones[:], 1.0)
+            nc.vector.memset(warm[:], 0.0)
+            make_identity(nc, ident[:])
+            nc.scalar.dma_start(out=scale_all[:], in_=x_scale.rearrange("o k -> (o k)").partition_broadcast(P))
+            nc.sync.dma_start(out=xb[0][:], in_=x_bytes[0:P, :])
+            c1v = c1.rearrange("(j m) k -> m j k", m=P)
+            c2v = c2.rearrange("(j m) k -> m j k", m=P)
+            v1v = v1.rearrange("(m t) k -> m t k", t=4)
+            nc.sync.dma_start(out=raw["c1"][:, 0:2, :], in_=c1v[:, 0:2, :])
+            nc.sync.dma_start(out=raw["c1"][:, 2:4, :], in_=c1v[:, 2:4, :])
+            for i in range(1, 4):
+                nc.sync.dma_start(out=xb[i][:], in_=x_bytes[P * i : P * (i + 1), :])
+            nc.scalar.dma_start(out=rows_b1[0:4, :], in_=b1.rearrange("(j p) -> j p", p=P))
+            nc.scalar.dma_start(out=rows_gb[0:1, 0, :], in_=g.rearrange("(o k) -> o k", o=1))
+            nc.scalar.dma_start(out=rows_gb[0:1, 1, :], in_=b2.rearrange("(o k) -> o k", o=1))
+            nc.sync.dma_start(out=raw["c2"][:, 0:2, :], in_=c2v[:, 0:2, :])
+            nc.sync.dma_start(out=raw["c2"][:, 2:4, :], in_=c2v[:, 2:4, :])
+            nc.sync.dma_start(out=xq4[0][:], in_=x_bytes[P * 4 : P * 8, :].rearrange("(i p) k -> p i k", p=P))
+            nc.sync.dma_start(out=raw["v1"][:, 0:2, :], in_=v1v[:, 0:2, :])
+            nc.sync.dma_start(out=raw["v1"][:, 2:4, :], in_=v1v[:, 2:4, :])
+            for q in (1, 2):
+                nc.sync.dma_start(out=xq4[q][:], in_=x_bytes[P * 4 * (q + 1) : P * 4 * (q + 2), :].rearrange("(i p) k -> p i k", p=P))
+            nc.scalar.activation(out=warm[:], in_=warm[:], func=ACT.Exp)
+
+            BANKS = {"c1": ("nz", "nz", "l2", "l2"), "c2": ("nz", "nz", "l2", "l2"), "v1": ("l2", "l2", "l2", "l2")}
+            BUFS = {"xt": 2, "nz": 2, "l2": 2, "s1": 1, "at": 1}
+
+            def bank(tag):
+                return psum.tile([P, 512], F32, name=tag, tag=tag, bufs=BUFS[tag])
+
+            st = {}
+
+            def head(op):
+                n = op[0:2]
+                kind = op[2:3]
+                if op == "gb":
+                    for h in range(2):
+                        ps = bank("l2")
+                        nc.tensor.matmul(out=ps[:], lhsT=ones[:], rhs=rows_gb[:, h, :], start=True, stop=True)
+                        if h == 0:
+                            nc.scalar.activation(out=neg_g[:], in_=ps[:], func=ACT.Copy, scale=-1.0)
+                        else:
+                            nc.scalar.copy(out=b2_all[:], in_=ps[:])
+                    return
+                if op == "b1":
+                    nc.vector.tensor_copy(out=rows_b1f[:], in_=rows_b1[:])
+                    ps = bank("s1")
+                    nc.tensor.transpose(ps[:, 0:P], rows_b1f[:], ident[:])
+                    nc.scalar.activation(out=neg_b1[:], in_=ps[:, 0:4], func=ACT.Copy, scale=-1.0)
+                    return
+                if op == "crq":
+                    nc.vector.quantize_mx(out=codes_cr[:].bitcast(FP8X4), scales=scl_cr[:], in_=grp_cr[:].rearrange("p n t -> p (n t)"))
+                    return
+                j = int(op[3])
+                if kind == "T":
+                    ps = bank(BANKS[n][j])
+                    words = raw[n][:, j, :].bitcast(F32)
+                    for gg in range(G):
+                        for u in range(2):
+                            c = 2 * gg + u
+                            nc.tensor.transpose(ps[:, P * c : P * (c + 1)], words[:, 256 * gg + u : 256 * (gg + 1) : 2], ident[:])
+                    st[n, j] = ps
+                elif kind == "e":
+                    ps = st.pop((n, j))
+                    src = ps[:].rearrange("p (g u r) -> p g r u", g=G, u=2)
+                    if n == "c2":
+                        dst = grp["c2"][:].rearrange("p g n t -> p g (n t)").bitcast(F32).rearrange("p g (n u) -> p g n u", u=2)[:, :, P * j : P * (j + 1), :]
+                    else:
+                        dst = grp[n][j][:].bitcast(F32).rearrange("p (g r u) -> p g r u", g=G, u=2)
+                    if op[4] == "v":
+                        nc.vector.tensor_copy(out=dst, in_=src)
+                    else:
+                        nc.scalar.copy(out=dst, in_=src)
+                elif kind == "q":
+                    if n == "c2":
+                        nc.vector.quantize_mx(out=codes[n][j][:].bitcast(FP8X4), scales=scl[n][j][:], in_=grp[n][:, j, :, :].rearrange("p n t -> p (n t)"))
+                    else:
+                        nc.vector.quantize_mx(out=codes[n][j][:].bitcast(FP8X4), scales=scl[n][j][:], in_=grp[n][j][:])
+            def cross(op):
+                j = int(op[3])
+                if op[2] == "m":
+                    ps = bank("l2")
+                    for t in range(4):
+                        for gg in range(G):
+                            nc.tensor.matmul_mx(
+                                out=ps[:, P * t : P * (t + 1)],
+                                lhsT=codes["v1"][t][:, P * gg : P * (gg + 1)].bitcast(FP8X4),
+                                lhsT_scale=scl["v1"][t][:, P * gg : P * (gg + 1)],
+                                rhs=codes["c2"][gg][:, P * j : P * (j + 1)].bitcast(FP8X4),
+                                rhs_scale=scl["c2"][gg][:, P * j : P * (j + 1)],
+                                start=(gg == 0), stop=(gg == G - 1))
+                    st["cr", j] = ps
+                else:
+                    ps = st.pop(("cr", j))
+                    nc.scalar.copy(out=grp_cr[:, P * j : P * (j + 1), :], in_=ps[:].rearrange("p (t n) -> p n t", t=4))
+
+            def stage(s, i):
+                if s == "B":
+                    xm = work.tile([P, D], BF16, name="xm", tag="xm", bufs=3)
+                    nc.vector.tensor_tensor(out=xm[:], in0=x_rows(i).bitcast(FP8), in1=scale_all[:], op=ALU.mult)
+                    st["xm", i] = xm
+                elif s == "C":
+                    xm = st.pop(("xm", i))
+                    ps = bank("xt")
+                    words = xm[:].bitcast(F32)
+                    for gg in range(G):
+                        for u in range(2):
+                            c = 2 * gg + u
+                            nc.tensor.transpose(ps[:, P * c : P * (c + 1)], words[:, 256 * gg + u : 256 * (gg + 1) : 2], ident[:])
+                    st["xt", i] = ps
+                elif s == "D":
+                    ps = st.pop(("xt", i))
+                    xg = work.tile([P, G * P * 4], BF16, name="xg", tag="xg", bufs=3, align_bytes=64)
+                    nc.scalar.copy(out=xg[:].bitcast(F32).rearrange("p (g r u) -> p g r u", g=G, u=2),
+                                   in_=ps[:].rearrange("p (g u r) -> p g r u", g=G, u=2))
+                    st["xg", i] = xg
+                elif s == "E":
+                    xg = st.pop(("xg", i))
+                    xc = work.tile([P, G * P], U32, name="xc", tag="xc", bufs=12, align_bytes=64)
+                    xs = work.tile([P, G * P], U8, name="xs", tag="xs", bufs=12, align_bytes=64)
+                    nc.vector.quantize_mx(out=xc[:].bitcast(FP8X4), scales=xs[:], in_=xg[:])
+                    st["xc", i] = (xc, xs)
+                elif s == "F":
+                    xc, xs = st["xc", i]
+                    ps = bank("s1")
+                    for j in range(4):
+                        for gg in range(G):
+                            nc.tensor.matmul_mx(
+                                out=ps[:, P * j : P * (j + 1)],
+                                lhsT=codes["c1"][j][:, P * gg : P * (gg + 1)].bitcast(FP8X4),
+                                lhsT_scale=scl["c1"][j][:, P * gg : P * (gg + 1)],
+                                rhs=xc[:, P * gg : P * (gg + 1)].bitcast(FP8X4),
+                                rhs_scale=xs[:, P * gg : P * (gg + 1)],
+                                start=(gg == 0), stop=(gg == G - 1))
+                    st["s1", i] = ps
+                elif s == "G":
+                    ps = st.pop(("s1", i))
+                    zt = work.tile([P, 4, P], F32, name="zt", tag="zt", bufs=3)
+                    for j in range(4):
+                        nc.scalar.activation(out=zt[:, j, :], in_=ps[:, P * j : P * (j + 1)], func=ACT.Identity, bias=neg_b1[:, j : j + 1], scale=-2.0)
+                    st["zt", i] = zt
+                elif s == "H":
+                    zt = st.pop(("zt", i))
+                    ps = bank("nz")
+                    for j in range(4):
+                        nc.tensor.transpose(ps[:, P * j : P * (j + 1)], zt[:, j, :], ident[:])
+                    st["nz", i] = ps
+                elif s == "I":
+                    mn = work.tile([P, 1], F32, name="mn", tag="mn", bufs=4)
+                    nc.vector.tensor_reduce(out=mn[:], in_=st["nz", i][:], axis=AX.X, op=ALU.min)
+                    st["mn", i] = mn
+                elif s == "J":
+                    ps = st.pop(("nz", i))
+                    mn = st.pop(("mn", i))
+                    e = work.tile([P, K], F32, name="e", tag="e", bufs=4)
+                    sm = work.tile([P, 1], F32, name="sm", tag="sm", bufs=4)
+                    nc.scalar.activation(out=e[:], in_=ps[:], func=ACT.Exp, bias=mn[:], scale=-1.0, accum_out=sm[:])
+                    st["e", i] = (e, sm)
+                elif s == "K":
+                    e, sm = st.pop(("e", i))
+                    rs = work.tile([P, 1], F32, name="rs", tag="rs", bufs=4)
+                    am = work.tile([P, K], BF16, name="am", tag="am", bufs=3)
+                    nc.vector.reciprocal(out=rs[:], in_=sm[:])
+                    nc.vector.scalar_tensor_tensor(out=am[:], in0=e[:], scalar=rs[:], in1=neg_g[:], op0=ALU.mult, op1=ALU.mult)
+                    st["am", i] = am
+                elif s == "L":
+                    am = st.pop(("am", i))
+                    ps = bank("at")
+                    words = am[:].bitcast(F32)
+                    for u in range(2):
+                        nc.tensor.transpose(ps[:, P * u : P * (u + 1)], words[:, u:256:2], ident[:])
+                    st["at", i] = ps
+                elif s == "M":
+                    ps = st.pop(("at", i))
+                    ag = work.tile([P, P * 4], BF16, name="ag", tag="ag", bufs=3, align_bytes=64)
+                    nc.scalar.copy(out=ag[:].bitcast(F32).rearrange("p (r u) -> p r u", u=2),
+                                   in_=ps[:, 0 : 2 * P].rearrange("p (u r) -> p r u", u=2))
+                    st["ag", i] = ag
+                elif s == "N":
+                    ag = st.pop(("ag", i))
+                    ac = work.tile([P, P], U32, name="ac", tag="ac", bufs=4, align_bytes=64)
+                    asc = work.tile([P, P], U8, name="asc", tag="asc", bufs=4, align_bytes=64)
+                    nc.vector.quantize_mx(out=ac[:].bitcast(FP8X4), scales=asc[:], in_=ag[:])
+                    st["ac", i] = (ac, asc)
+                elif s == "O":
+                    xc, xs = st.pop(("xc", i))
+                    ac, asc = st.pop(("ac", i))
+                    ps = bank("l2")
+                    for gg in range(G):
+                        nc.tensor.matmul_mx(out=ps[:], lhsT=xc[:, P * gg : P * (gg + 1)].bitcast(FP8X4), lhsT_scale=xs[:, P * gg : P * (gg + 1)],
+                                            rhs=codes["c2"][gg][:].bitcast(FP8X4), rhs_scale=scl["c2"][gg][:], start=(gg == 0), stop=False)
+                    nc.tensor.matmul_mx(out=ps[:], lhsT=ac[:].bitcast(FP8X4), lhsT_scale=asc[:],
+                                        rhs=codes_cr[:].bitcast(FP8X4), rhs_scale=scl_cr[:], start=False, stop=True)
+                    st["l2", i] = ps
+                elif s == "P":
+                    ps = st.pop(("l2", i))
+                    nc.vector.scalar_tensor_tensor(out=ny[i][:], in0=ps[:], scalar=-1.0, in1=b2_all[:], op0=ALU.mult, op1=ALU.subtract)
+                elif s == "Q":
+                    hi, c = group(i)
+                    nc.vector.tensor_reduce(out=min2[hi][:, c : c + 1], in_=ny[i][:], axis=AX.X, op=ALU.min)
+                elif s == "R":
+                    hi, c = group(i)
+                    junk = work.tile([P, M], BF16, name="junk", tag="junk", bufs=2)
+                    nc.scalar.activation(out=junk[:], in_=ny[i][:], func=ACT.Exp, bias=min2[hi][:, c : c + 1], scale=-1.0, accum_out=sum2[hi][:, c : c + 1])
+
+            def finish(i, engine):
+                hi, c = group(i)
+                ob = work.tile([P, M], F32, name="ob", tag="ob", bufs=4)
+                if engine == "s":
+                    nc.scalar.activation(out=ob[:], in_=ny[i][:], func=ACT.Identity, bias=shift[hi][:, c : c + 1], scale=-1.0)
+                else:
+                    nc.vector.tensor_scalar(out=ob[:], in0=ny[i][:], scalar1=-1.0, scalar2=shift[hi][:, c : c + 1], op0=ALU.mult, op1=ALU.add)
+                nc.sync.dma_start(out=out[P * i : P * (i + 1), :], in_=ob[:])
+
+            head("b1")
+            pending = []
+            for s in range(NT + OFFSET["R"]):
+                for op in HEAD.get(s, []):
+                    if op[0:3] in ("crm", "cre"):
+                        cross(op)
+                    else:
+                        head(op)
+                for c in ORDER:
+                    i = s - OFFSET[c]
+                    if i < 0 or i >= NT:
+                        continue
+                    stage(c, i)
+                    if c == "R" and i in GROUPS:
+                        nc.scalar.activation(out=lns[i][:], in_=sum2[i][:], func=ACT.Ln, scale=1.0 / M)
+                        nc.vector.tensor_sub(out=shift[i][:], in0=min2[i][:], in1=lns[i][:])
+                        lo = ([-1] + [h for h in GROUPS if h < i])[-1] + 1
+                        pending.extend(range(lo, i + 1))
+                        if i == NT - 1:
+                            for n, r in enumerate(pending):
+                                finish(r, "vs"[n % 2])
+                            pending = []
+                if s > OFFSET["R"] + GROUPS[0]:
+                    for r in pending[0:2]:
+                        finish(r, "s")
+                    pending = pending[2:]

@@ -20,23 +20,23 @@ P = 128
 NT = B // P
 G = D // 512
 
-ORDER = "OKFGBHJPELDNQIMCR"
-OFFSET = {"B": 0, "C": 1, "D": 2, "E": 3, "F": 5, "G": 5, "H": 6, "I": 6, "J": 7,
-          "K": 9, "L": 9, "M": 9, "N": 10, "O": 12, "P": 12, "Q": 12, "R": 12}
+ORDER = "OLBQMNFDIKEHRPGCkJ"
+OFFSET = {"B": 0, "C": 1, "D": 2, "E": 3, "F": 6, "G": 6, "H": 7, "I": 8, "J": 8, "k": 9, "K": 10, "L": 11, "M": 11, "N": 12, "O": 13, "P": 13, "Q": 14, "R": 14}
 HEAD = {
-    2: ["c1T0", "c1T1", "c1T2", "c1T3"],
-    3: ["c1e0s", "c1e1v", "c1e2s", "c1e3v", "c2T0", "c2T1", "c2e0s", "c2e1s"],
-    4: ["c1q0", "c1q1", "c1q2", "c1q3", "c2T2", "c2T3", "c2e2s", "c2e3s"],
-    5: ["v1T0", "v1T1", "v1e0s", "v1e1s"],
-    6: ["c2q0", "c2q1", "v1q0", "v1q1", "v1T2", "v1T3", "v1e2s", "v1e3s"],
-    7: ["gb"],
-    8: ["v1q2", "v1q3"],
-    9: ["crm0", "cre0s"],
-    10: ["crm1", "cre1s", "crm2", "cre2s"],
-    11: ["crm3", "cre3s"],
-    12: ["crq"],
+    2: ["c1T1", "c1T0", "c1T2"],
+    3: ["c1e0s", "c1e1v"],
+    4: ["c1e2s", "c2T0", "c2e0s", "c1q1"],
+    5: ["c1T3", "c2T2", "c1e3s"],
+    6: ["c2T1", "v1T0", "c2e2s", "v1e0s", "c2T3", "c1q3", "v1T2", "c1q2", "c1q0", "c2e3s", "v1e2s", "c2e1v"],
+    7: ["v1T1", "v1T3", "v1q0", "v1q2", "v1e1s"],
+    8: ["v1e3s"],
+    9: ["c2q1", "c2q0", "v1q1", "v1q3", "gb"],
+    10: ["crm0", "crm1", "cre0s"],
+    11: ["cre1s"],
+    12: ["crm2", "cre2s", "crm3", "cre3s"],
+    13: ["crq"],
 }
-GROUPS = (9, 15)
+GROUPS = (10, 15)
 
 
 def tile_softresidualsemanticids_kernel(tc, x_bytes, x_scale, c1, v1, c2, g, b1, b2, out):
@@ -106,28 +106,26 @@ def tile_softresidualsemanticids_kernel(tc, x_bytes, x_scale, c1, v1, c2, g, b1,
             nc.gpsimd.memset(ones[:], 1.0)
             nc.vector.memset(warm[:], 0.0)
             make_identity(nc, ident[:])
-            nc.scalar.dma_start(out=scale_all[:], in_=x_scale.rearrange("o k -> (o k)").partition_broadcast(P))
-            nc.sync.dma_start(out=xb[0][:], in_=x_bytes[0:P, :])
-            c1v = c1.rearrange("(j m) k -> m j k", m=P)
-            c2v = c2.rearrange("(j m) k -> m j k", m=P)
-            v1v = v1.rearrange("(m t) k -> m t k", t=4)
-            nc.sync.dma_start(out=raw["c1"][:, 0:2, :], in_=c1v[:, 0:2, :])
-            nc.sync.dma_start(out=raw["c1"][:, 2:4, :], in_=c1v[:, 2:4, :])
-            for i in range(1, 4):
-                nc.sync.dma_start(out=xb[i][:], in_=x_bytes[P * i : P * (i + 1), :])
+            nc.sync.dma_start(out=scale_all[:], in_=x_scale.rearrange("o k -> (o k)").partition_broadcast(P))
             nc.scalar.dma_start(out=rows_b1[0:4, :], in_=b1.rearrange("(j p) -> j p", p=P))
             nc.scalar.dma_start(out=rows_gb[0:1, 0, :], in_=g.rearrange("(o k) -> o k", o=1))
             nc.scalar.dma_start(out=rows_gb[0:1, 1, :], in_=b2.rearrange("(o k) -> o k", o=1))
-            nc.sync.dma_start(out=raw["c2"][:, 0:2, :], in_=c2v[:, 0:2, :])
-            nc.sync.dma_start(out=raw["c2"][:, 2:4, :], in_=c2v[:, 2:4, :])
+            c1v = c1.rearrange("(j m) k -> m j k", m=P)
+            c2v = c2.rearrange("(j m) k -> m j k", m=P)
+            v1v = v1.rearrange("(m t) k -> m t k", t=4)
+            for i in range(4):
+                nc.sync.dma_start(out=xb[i][:], in_=x_bytes[P * i : P * (i + 1), :])
+            for n, view in (("c1", c1v), ("c2", c2v)):
+                for h in (0, 2):
+                    nc.sync.dma_start(out=raw[n][:, h : h + 2, :], in_=view[:, h : h + 2, :])
             nc.sync.dma_start(out=xq4[0][:], in_=x_bytes[P * 4 : P * 8, :].rearrange("(i p) k -> p i k", p=P))
-            nc.sync.dma_start(out=raw["v1"][:, 0:2, :], in_=v1v[:, 0:2, :])
-            nc.sync.dma_start(out=raw["v1"][:, 2:4, :], in_=v1v[:, 2:4, :])
+            for h in (0, 2):
+                nc.sync.dma_start(out=raw["v1"][:, h : h + 2, :], in_=v1v[:, h : h + 2, :])
             for q in (1, 2):
                 nc.sync.dma_start(out=xq4[q][:], in_=x_bytes[P * 4 * (q + 1) : P * 4 * (q + 2), :].rearrange("(i p) k -> p i k", p=P))
             nc.scalar.activation(out=warm[:], in_=warm[:], func=ACT.Exp)
 
-            BANKS = {"c1": ("nz", "nz", "l2", "l2"), "c2": ("nz", "nz", "l2", "l2"), "v1": ("l2", "l2", "l2", "l2")}
+            BANKS = {"c1": ("nz", "nz", "l2", "l2"), "c2": ("nz", "nz", "l2", "l2"), "v1": ("l2", "l2", "at", "at")}
             BUFS = {"xt": 2, "nz": 2, "l2": 2, "s1": 1, "at": 1}
 
             def bank(tag):
@@ -201,7 +199,7 @@ def tile_softresidualsemanticids_kernel(tc, x_bytes, x_scale, c1, v1, c2, g, b1,
 
             def stage(s, i):
                 if s == "B":
-                    xm = work.tile([P, D], BF16, name="xm", tag="xm", bufs=3)
+                    xm = work.tile([P, D], BF16, name="xm", tag="xm", bufs=4)
                     nc.vector.tensor_tensor(out=xm[:], in0=x_rows(i).bitcast(FP8), in1=scale_all[:], op=ALU.mult)
                     st["xm", i] = xm
                 elif s == "C":
@@ -221,8 +219,8 @@ def tile_softresidualsemanticids_kernel(tc, x_bytes, x_scale, c1, v1, c2, g, b1,
                     st["xg", i] = xg
                 elif s == "E":
                     xg = st.pop(("xg", i))
-                    xc = work.tile([P, G * P], U32, name="xc", tag="xc", bufs=12, align_bytes=64)
-                    xs = work.tile([P, G * P], U8, name="xs", tag="xs", bufs=12, align_bytes=64)
+                    xc = work.tile([P, G * P], U32, name="xc", tag="xc", bufs=13, align_bytes=64)
+                    xs = work.tile([P, G * P], U8, name="xs", tag="xs", bufs=13, align_bytes=64)
                     nc.vector.quantize_mx(out=xc[:].bitcast(FP8X4), scales=xs[:], in_=xg[:])
                     st["xc", i] = (xc, xs)
                 elif s == "F":
@@ -257,15 +255,20 @@ def tile_softresidualsemanticids_kernel(tc, x_bytes, x_scale, c1, v1, c2, g, b1,
                 elif s == "J":
                     ps = st.pop(("nz", i))
                     mn = st.pop(("mn", i))
-                    e = work.tile([P, K], F32, name="e", tag="e", bufs=4)
-                    sm = work.tile([P, 1], F32, name="sm", tag="sm", bufs=4)
+                    e = work.tile([P, K], F32, name="e", tag="e", bufs=5)
+                    sm = work.tile([P, 1], F32, name="sm", tag="sm", bufs=5)
                     nc.scalar.activation(out=e[:], in_=ps[:], func=ACT.Exp, bias=mn[:], scale=-1.0, accum_out=sm[:])
-                    st["e", i] = (e, sm)
-                elif s == "K":
-                    e, sm = st.pop(("e", i))
+                    st["e", i] = e
+                    st["sm", i] = sm
+                elif s == "k":
+                    sm = st.pop(("sm", i))
                     rs = work.tile([P, 1], F32, name="rs", tag="rs", bufs=4)
-                    am = work.tile([P, K], BF16, name="am", tag="am", bufs=3)
                     nc.vector.reciprocal(out=rs[:], in_=sm[:])
+                    st["rs", i] = rs
+                elif s == "K":
+                    e = st.pop(("e", i))
+                    rs = st.pop(("rs", i))
+                    am = work.tile([P, K], BF16, name="am", tag="am", bufs=3)
                     nc.vector.scalar_tensor_tensor(out=am[:], in0=e[:], scalar=rs[:], in1=neg_g[:], op0=ALU.mult, op1=ALU.mult)
                     st["am", i] = am
                 elif s == "L":
@@ -332,7 +335,7 @@ def tile_softresidualsemanticids_kernel(tc, x_bytes, x_scale, c1, v1, c2, g, b1,
                     stage(c, i)
                     if c == "R" and i in GROUPS:
                         nc.scalar.activation(out=lns[i][:], in_=sum2[i][:], func=ACT.Ln, scale=1.0 / M)
-                        nc.vector.tensor_sub(out=shift[i][:], in0=min2[i][:], in1=lns[i][:])
+                        (nc.vector if i == NT - 1 else nc.gpsimd).tensor_sub(out=shift[i][:], in0=min2[i][:], in1=lns[i][:])
                         lo = ([-1] + [h for h in GROUPS if h < i])[-1] + 1
                         pending.extend(range(lo, i + 1))
                         if i == NT - 1:
@@ -340,6 +343,6 @@ def tile_softresidualsemanticids_kernel(tc, x_bytes, x_scale, c1, v1, c2, g, b1,
                                 finish(r, "vs"[n % 2])
                             pending = []
                 if s > OFFSET["R"] + GROUPS[0]:
-                    for r in pending[0:2]:
+                    for r in pending[0:1]:
                         finish(r, "s")
-                    pending = pending[2:]
+                    pending = pending[1:]

from contextlib import ExitStack

import concourse.mybir as mybir
from concourse.masks import make_identity

B, D, K, M = 2048, 1024, 512, 512
FLOPS = 2 * B * D * (K + M) + 2 * K * M * D + 2 * B * K * M

F32 = mybir.dt.float32
BF16 = mybir.dt.bfloat16
U32 = mybir.dt.uint32
U8 = mybir.dt.uint8
FP8 = mybir.dt.float8_e4m3fn
FP8X4 = mybir.dt.float8_e4m3fn_x4
ACT = mybir.ActivationFunctionType
ALU = mybir.AluOpType
AX = mybir.AxisListType

P = 128
NT = B // P
G = D // 512

ORDER = "OLBQMNFDIKEHRPGCkJ"
OFFSET = {"B": 0, "C": 1, "D": 2, "E": 3, "F": 6, "G": 6, "H": 7, "I": 8, "J": 8, "k": 9, "K": 10, "L": 11, "M": 11, "N": 12, "O": 13, "P": 13, "Q": 14, "R": 14}
HEAD = {
    2: ["c1T1", "c1T0", "c1T2"],
    3: ["c1e0s", "c1e1v"],
    4: ["c1e2s", "c2T0", "c2e0s", "c1q1"],
    5: ["c1T3", "c2T2", "c1e3s"],
    6: ["c2T1", "v1T0", "c2e2s", "v1e0s", "c2T3", "c1q3", "v1T2", "c1q2", "c1q0", "c2e3s", "v1e2s", "c2e1v"],
    7: ["v1T1", "v1T3", "v1q0", "v1q2", "v1e1s"],
    8: ["v1e3s"],
    9: ["c2q1", "c2q0", "v1q1", "v1q3", "gb"],
    10: ["crm0", "crm1", "cre0s"],
    11: ["cre1s"],
    12: ["crm2", "cre2s", "crm3", "cre3s"],
    13: ["crq"],
}
GROUPS = (10, 15)


def tile_softresidualsemanticids_kernel(tc, x_bytes, x_scale, c1, v1, c2, g, b1, b2, out):
    nc = tc.nc
    with ExitStack() as ctx:
        keep = ctx.enter_context(tc.tile_pool(name="keep", bufs=1))
        work = ctx.enter_context(tc.tile_pool(name="work", bufs=3))
        psum = ctx.enter_context(tc.psum_pool(name="psum", bufs=1))

        ident = keep.tile([P, P], F32, name="ident")
        ones = keep.tile([P, P], BF16, name="ones")
        rows_gb = keep.tile([P, 2, K], BF16, name="rows_gb")
        rows_b1 = keep.tile([P, P], BF16, name="rows_b1")
        rows_b1f = keep.tile([P, P], F32, name="rows_b1f")
        neg_b1 = keep.tile([P, 4], F32, name="neg_b1")
        neg_g = keep.tile([P, K], BF16, name="neg_g")
        b2_all = keep.tile([P, M], BF16, name="b2_all")
        scale_all = keep.tile([P, D], F32, name="scale_all")
        warm = keep.tile([P, 1], F32, name="warm")
        xb = [keep.tile([P, D], U8, name="xb%d" % i) for i in range(4)]
        xq4 = [keep.tile([P, 4, D], U8, name="xbq%d" % i) for i in range(3)]
        raw = {}
        for n in ("c1", "c2", "v1"):
            raw[n] = keep.tile([P, 4, D], BF16, name="raw_" + n)
        grp = {}
        codes = {}
        scl = {}
        for n in ("c1", "v1"):
            grp[n] = [keep.tile([P, G * P * 4], BF16, name="grp_%s%d" % (n, j), align_bytes=64) for j in range(4)]
            codes[n] = [keep.tile([P, G * P], U32, name="codes_%s%d" % (n, j), align_bytes=64) for j in range(4)]
            scl[n] = [keep.tile([P, G * P], U8, name="scl_%s%d" % (n, j), align_bytes=64) for j in range(4)]
        grp["c2"] = keep.tile([P, G, M, 4], BF16, name="grp_c2", align_bytes=64)
        codes["c2"] = [keep.tile([P, M], U32, name="codes_c2%d" % j, align_bytes=64) for j in range(G)]
        scl["c2"] = [keep.tile([P, M], U8, name="scl_c2%d" % j, align_bytes=64) for j in range(G)]
        grp_cr = keep.tile([P, M, 4], BF16, name="grp_cr", align_bytes=64)
        codes_cr = keep.tile([P, M], U32, name="codes_cr", align_bytes=64)
        scl_cr = keep.tile([P, M], U8, name="scl_cr", align_bytes=64)
        ny = [keep.tile([P, M], F32, name="ny%d" % i) for i in range(NT)]
        sum2 = {}
        min2 = {}
        lns = {}
        shift = {}
        lo = 0
        for hi in GROUPS:
            n = hi + 1 - lo
            sum2[hi] = keep.tile([P, n], F32, name="sum2_%d" % hi)
            min2[hi] = keep.tile([P, n], F32, name="min2_%d" % hi)
            lns[hi] = keep.tile([P, n], F32, name="lns_%d" % hi)
            shift[hi] = keep.tile([P, n], F32, name="shift_%d" % hi)
            lo = hi + 1

        def group(i):
            lo = 0
            for hi in GROUPS:
                if i <= hi:
                    return hi, i - lo
                lo = hi + 1

        def x_rows(i):
            if i < 4:
                return xb[i][:]
            return xq4[i // 4 - 1][:, i % 4, :]

        with tc.manual_schedule():
            nc.gpsimd.memset(rows_gb[:], 0.0)
            nc.gpsimd.memset(rows_b1[:], 0.0)
            nc.gpsimd.memset(ones[:], 1.0)
            nc.vector.memset(warm[:], 0.0)
            make_identity(nc, ident[:])
            nc.sync.dma_start(out=scale_all[:], in_=x_scale.rearrange("o k -> (o k)").partition_broadcast(P))
            nc.scalar.dma_start(out=rows_b1[0:4, :], in_=b1.rearrange("(j p) -> j p", p=P))
            nc.scalar.dma_start(out=rows_gb[0:1, 0, :], in_=g.rearrange("(o k) -> o k", o=1))
            nc.scalar.dma_start(out=rows_gb[0:1, 1, :], in_=b2.rearrange("(o k) -> o k", o=1))
            c1v = c1.rearrange("(j m) k -> m j k", m=P)
            c2v = c2.rearrange("(j m) k -> m j k", m=P)
            v1v = v1.rearrange("(m t) k -> m t k", t=4)
            for i in range(4):
                nc.sync.dma_start(out=xb[i][:], in_=x_bytes[P * i : P * (i + 1), :])
            for n, view in (("c1", c1v), ("c2", c2v)):
                for h in (0, 2):
                    nc.sync.dma_start(out=raw[n][:, h : h + 2, :], in_=view[:, h : h + 2, :])
            nc.sync.dma_start(out=xq4[0][:], in_=x_bytes[P * 4 : P * 8, :].rearrange("(i p) k -> p i k", p=P))
            for h in (0, 2):
                nc.sync.dma_start(out=raw["v1"][:, h : h + 2, :], in_=v1v[:, h : h + 2, :])
            for q in (1, 2):
                nc.sync.dma_start(out=xq4[q][:], in_=x_bytes[P * 4 * (q + 1) : P * 4 * (q + 2), :].rearrange("(i p) k -> p i k", p=P))
            nc.scalar.activation(out=warm[:], in_=warm[:], func=ACT.Exp)

            BANKS = {"c1": ("nz", "nz", "l2", "l2"), "c2": ("nz", "nz", "l2", "l2"), "v1": ("l2", "l2", "at", "at")}
            BUFS = {"xt": 2, "nz": 2, "l2": 2, "s1": 1, "at": 1}

            def bank(tag):
                return psum.tile([P, 512], F32, name=tag, tag=tag, bufs=BUFS[tag])

            st = {}

            def head(op):
                n = op[0:2]
                kind = op[2:3]
                if op == "gb":
                    for h in range(2):
                        ps = bank("l2")
                        nc.tensor.matmul(out=ps[:], lhsT=ones[:], rhs=rows_gb[:, h, :], start=True, stop=True)
                        if h == 0:
                            nc.scalar.activation(out=neg_g[:], in_=ps[:], func=ACT.Copy, scale=-1.0)
                        else:
                            nc.scalar.copy(out=b2_all[:], in_=ps[:])
                    return
                if op == "b1":
                    nc.vector.tensor_copy(out=rows_b1f[:], in_=rows_b1[:])
                    ps = bank("s1")
                    nc.tensor.transpose(ps[:, 0:P], rows_b1f[:], ident[:])
                    nc.scalar.activation(out=neg_b1[:], in_=ps[:, 0:4], func=ACT.Copy, scale=-1.0)
                    return
                if op == "crq":
                    nc.vector.quantize_mx(out=codes_cr[:].bitcast(FP8X4), scales=scl_cr[:], in_=grp_cr[:].rearrange("p n t -> p (n t)"))
                    return
                j = int(op[3])
                if kind == "T":
                    ps = bank(BANKS[n][j])
                    words = raw[n][:, j, :].bitcast(F32)
                    for gg in range(G):
                        for u in range(2):
                            c = 2 * gg + u
                            nc.tensor.transpose(ps[:, P * c : P * (c + 1)], words[:, 256 * gg + u : 256 * (gg + 1) : 2], ident[:])
                    st[n, j] = ps
                elif kind == "e":
                    ps = st.pop((n, j))
                    src = ps[:].rearrange("p (g u r) -> p g r u", g=G, u=2)
                    if n == "c2":
                        dst = grp["c2"][:].rearrange("p g n t -> p g (n t)").bitcast(F32).rearrange("p g (n u) -> p g n u", u=2)[:, :, P * j : P * (j + 1), :]
                    else:
                        dst = grp[n][j][:].bitcast(F32).rearrange("p (g r u) -> p g r u", g=G, u=2)
                    if op[4] == "v":
                        nc.vector.tensor_copy(out=dst, in_=src)
                    else:
                        nc.scalar.copy(out=dst, in_=src)
                elif kind == "q":
                    if n == "c2":
                        nc.vector.quantize_mx(out=codes[n][j][:].bitcast(FP8X4), scales=scl[n][j][:], in_=grp[n][:, j, :, :].rearrange("p n t -> p (n t)"))
                    else:
                        nc.vector.quantize_mx(out=codes[n][j][:].bitcast(FP8X4), scales=scl[n][j][:], in_=grp[n][j][:])
            def cross(op):
                j = int(op[3])
                if op[2] == "m":
                    ps = bank("l2")
                    for t in range(4):
                        for gg in range(G):
                            nc.tensor.matmul_mx(
                                out=ps[:, P * t : P * (t + 1)],
                                lhsT=codes["v1"][t][:, P * gg : P * (gg + 1)].bitcast(FP8X4),
                                lhsT_scale=scl["v1"][t][:, P * gg : P * (gg + 1)],
                                rhs=codes["c2"][gg][:, P * j : P * (j + 1)].bitcast(FP8X4),
                                rhs_scale=scl["c2"][gg][:, P * j : P * (j + 1)],
                                start=(gg == 0), stop=(gg == G - 1))
                    st["cr", j] = ps
                else:
                    ps = st.pop(("cr", j))
                    nc.scalar.copy(out=grp_cr[:, P * j : P * (j + 1), :], in_=ps[:].rearrange("p (t n) -> p n t", t=4))

            def stage(s, i):
                if s == "B":
                    xm = work.tile([P, D], BF16, name="xm", tag="xm", bufs=4)
                    nc.vector.tensor_tensor(out=xm[:], in0=x_rows(i).bitcast(FP8), in1=scale_all[:], op=ALU.mult)
                    st["xm", i] = xm
                elif s == "C":
                    xm = st.pop(("xm", i))
                    ps = bank("xt")
                    words = xm[:].bitcast(F32)
                    for gg in range(G):
                        for u in range(2):
                            c = 2 * gg + u
                            nc.tensor.transpose(ps[:, P * c : P * (c + 1)], words[:, 256 * gg + u : 256 * (gg + 1) : 2], ident[:])
                    st["xt", i] = ps
                elif s == "D":
                    ps = st.pop(("xt", i))
                    xg = work.tile([P, G * P * 4], BF16, name="xg", tag="xg", bufs=3, align_bytes=64)
                    nc.scalar.copy(out=xg[:].bitcast(F32).rearrange("p (g r u) -> p g r u", g=G, u=2),
                                   in_=ps[:].rearrange("p (g u r) -> p g r u", g=G, u=2))
                    st["xg", i] = xg
                elif s == "E":
                    xg = st.pop(("xg", i))
                    xc = work.tile([P, G * P], U32, name="xc", tag="xc", bufs=13, align_bytes=64)
                    xs = work.tile([P, G * P], U8, name="xs", tag="xs", bufs=13, align_bytes=64)
                    nc.vector.quantize_mx(out=xc[:].bitcast(FP8X4), scales=xs[:], in_=xg[:])
                    st["xc", i] = (xc, xs)
                elif s == "F":
                    xc, xs = st["xc", i]
                    ps = bank("s1")
                    for j in range(4):
                        for gg in range(G):
                            nc.tensor.matmul_mx(
                                out=ps[:, P * j : P * (j + 1)],
                                lhsT=codes["c1"][j][:, P * gg : P * (gg + 1)].bitcast(FP8X4),
                                lhsT_scale=scl["c1"][j][:, P * gg : P * (gg + 1)],
                                rhs=xc[:, P * gg : P * (gg + 1)].bitcast(FP8X4),
                                rhs_scale=xs[:, P * gg : P * (gg + 1)],
                                start=(gg == 0), stop=(gg == G - 1))
                    st["s1", i] = ps
                elif s == "G":
                    ps = st.pop(("s1", i))
                    zt = work.tile([P, 4, P], F32, name="zt", tag="zt", bufs=3)
                    for j in range(4):
                        nc.scalar.activation(out=zt[:, j, :], in_=ps[:, P * j : P * (j + 1)], func=ACT.Identity, bias=neg_b1[:, j : j + 1], scale=-2.0)
                    st["zt", i] = zt
                elif s == "H":
                    zt = st.pop(("zt", i))
                    ps = bank("nz")
                    for j in range(4):
                        nc.tensor.transpose(ps[:, P * j : P * (j + 1)], zt[:, j, :], ident[:])
                    st["nz", i] = ps
                elif s == "I":
                    mn = work.tile([P, 1], F32, name="mn", tag="mn", bufs=4)
                    nc.vector.tensor_reduce(out=mn[:], in_=st["nz", i][:], axis=AX.X, op=ALU.min)
                    st["mn", i] = mn
                elif s == "J":
                    ps = st.pop(("nz", i))
                    mn = st.pop(("mn", i))
                    e = work.tile([P, K], F32, name="e", tag="e", bufs=5)
                    sm = work.tile([P, 1], F32, name="sm", tag="sm", bufs=5)
                    nc.scalar.activation(out=e[:], in_=ps[:], func=ACT.Exp, bias=mn[:], scale=-1.0, accum_out=sm[:])
                    st["e", i] = e
                    st["sm", i] = sm
                elif s == "k":
                    sm = st.pop(("sm", i))
                    rs = work.tile([P, 1], F32, name="rs", tag="rs", bufs=4)
                    nc.vector.reciprocal(out=rs[:], in_=sm[:])
                    st["rs", i] = rs
                elif s == "K":
                    e = st.pop(("e", i))
                    rs = st.pop(("rs", i))
                    am = work.tile([P, K], BF16, name="am", tag="am", bufs=3)
                    nc.vector.scalar_tensor_tensor(out=am[:], in0=e[:], scalar=rs[:], in1=neg_g[:], op0=ALU.mult, op1=ALU.mult)
                    st["am", i] = am
                elif s == "L":
                    am = st.pop(("am", i))
                    ps = bank("at")
                    words = am[:].bitcast(F32)
                    for u in range(2):
                        nc.tensor.transpose(ps[:, P * u : P * (u + 1)], words[:, u:256:2], ident[:])
                    st["at", i] = ps
                elif s == "M":
                    ps = st.pop(("at", i))
                    ag = work.tile([P, P * 4], BF16, name="ag", tag="ag", bufs=3, align_bytes=64)
                    nc.scalar.copy(out=ag[:].bitcast(F32).rearrange("p (r u) -> p r u", u=2),
                                   in_=ps[:, 0 : 2 * P].rearrange("p (u r) -> p r u", u=2))
                    st["ag", i] = ag
                elif s == "N":
                    ag = st.pop(("ag", i))
                    ac = work.tile([P, P], U32, name="ac", tag="ac", bufs=4, align_bytes=64)
                    asc = work.tile([P, P], U8, name="asc", tag="asc", bufs=4, align_bytes=64)
                    nc.vector.quantize_mx(out=ac[:].bitcast(FP8X4), scales=asc[:], in_=ag[:])
                    st["ac", i] = (ac, asc)
                elif s == "O":
                    xc, xs = st.pop(("xc", i))
                    ac, asc = st.pop(("ac", i))
                    ps = bank("l2")
                    for gg in range(G):
                        nc.tensor.matmul_mx(out=ps[:], lhsT=xc[:, P * gg : P * (gg + 1)].bitcast(FP8X4), lhsT_scale=xs[:, P * gg : P * (gg + 1)],
                                            rhs=codes["c2"][gg][:].bitcast(FP8X4), rhs_scale=scl["c2"][gg][:], start=(gg == 0), stop=False)
                    nc.tensor.matmul_mx(out=ps[:], lhsT=ac[:].bitcast(FP8X4), lhsT_scale=asc[:],
                                        rhs=codes_cr[:].bitcast(FP8X4), rhs_scale=scl_cr[:], start=False, stop=True)
                    st["l2", i] = ps
                elif s == "P":
                    ps = st.pop(("l2", i))
                    nc.vector.scalar_tensor_tensor(out=ny[i][:], in0=ps[:], scalar=-1.0, in1=b2_all[:], op0=ALU.mult, op1=ALU.subtract)
                elif s == "Q":
                    hi, c = group(i)
                    nc.vector.tensor_reduce(out=min2[hi][:, c : c + 1], in_=ny[i][:], axis=AX.X, op=ALU.min)
                elif s == "R":
                    hi, c = group(i)
                    junk = work.tile([P, M], BF16, name="junk", tag="junk", bufs=2)
                    nc.scalar.activation(out=junk[:], in_=ny[i][:], func=ACT.Exp, bias=min2[hi][:, c : c + 1], scale=-1.0, accum_out=sum2[hi][:, c : c + 1])

            def finish(i, engine):
                hi, c = group(i)
                ob = work.tile([P, M], F32, name="ob", tag="ob", bufs=4)
                if engine == "s":
                    nc.scalar.activation(out=ob[:], in_=ny[i][:], func=ACT.Identity, bias=shift[hi][:, c : c + 1], scale=-1.0)
                else:
                    nc.vector.tensor_scalar(out=ob[:], in0=ny[i][:], scalar1=-1.0, scalar2=shift[hi][:, c : c + 1], op0=ALU.mult, op1=ALU.add)
                nc.sync.dma_start(out=out[P * i : P * (i + 1), :], in_=ob[:])

            head("b1")
            pending = []
            for s in range(NT + OFFSET["R"]):
                for op in HEAD.get(s, []):
                    if op[0:3] in ("crm", "cre"):
                        cross(op)
                    else:
                        head(op)
                for c in ORDER:
                    i = s - OFFSET[c]
                    if i < 0 or i >= NT:
                        continue
                    stage(c, i)
                    if c == "R" and i in GROUPS:
                        nc.scalar.activation(out=lns[i][:], in_=sum2[i][:], func=ACT.Ln, scale=1.0 / M)
                        (nc.vector if i == NT - 1 else nc.gpsimd).tensor_sub(out=shift[i][:], in0=min2[i][:], in1=lns[i][:])
                        lo = ([-1] + [h for h in GROUPS if h < i])[-1] + 1
                        pending.extend(range(lo, i + 1))
                        if i == NT - 1:
                            for n, r in enumerate(pending):
                                finish(r, "vs"[n % 2])
                            pending = []
                if s > OFFSET["R"] + GROUPS[0]:
                    for r in pending[0:1]:
                        finish(r, "s")
                    pending = pending[1:]
